import numpy as np
import ml_dtypes


def mxq(x, axis, fmt="e4m3"):
    dtype, down = {"e4m3": (ml_dtypes.float8_e4m3fn, 7), "e5m2": (ml_dtypes.float8_e5m2, 14)}[fmt]
    v = np.moveaxis(np.asarray(x, np.float32).astype(ml_dtypes.bfloat16).astype(np.float64), axis, -1)
    blocks = v.reshape(v.shape[:-1] + (-1, 32))
    amax = np.abs(blocks).max(-1, keepdims=True)
    byte = np.maximum(np.where(amax > 0, np.frexp(amax)[1] - 1 + 127, 0) - down, 1)
    scale = np.exp2(byte - 127.0)
    codes = (blocks / scale).astype(np.float32).astype(dtype).astype(np.float64)
    return np.moveaxis((codes * scale).reshape(v.shape), -1, axis)


WIDE = False


def mx_kscale(k):
    if not WIDE:
        return np.ones(k)
    levels = np.array([10, -10, 5, -5, 0])
    if k % 512:
        return np.exp2(np.random.permutation(np.resize(levels, k // 32))).repeat(32)
    a = np.empty((k // 512, 16))
    for p in range(k // 512):
        a[p, :8] = np.random.permutation(np.resize(levels, 8))
        for g in range(8):
            far = levels[np.abs(levels - a[p, g]) >= 10]
            a[p, g + 8] = far[np.random.randint(len(far))]
    return np.exp2(a.ravel()).repeat(32)


def f64(x):
    return np.asarray(x).astype(np.float64)


def striped(idx):
    return np.tile(idx.reshape(-1, 16).T, (8, 1)).astype(np.uint16)


def unstriped(offs):
    return offs[:16].T.reshape(-1).astype(np.int64)


E2M1 = np.array([0.0, 0.5, 1.0, 1.5, 2.0, 3.0, 4.0, 6.0, -0.0, -0.5, -1.0, -1.5, -2.0, -3.0, -4.0, -6.0])


def pack_weight(w, fmt):
    k, n = w.shape
    w = f64(np.asarray(w, np.float32).astype(ml_dtypes.bfloat16)).reshape(k // 32, 32, n)
    amax = np.abs(w).max(1)
    if fmt == "e4m3":
        byte = np.frexp(amax)[1] - 1 + 127 - 7
    else:
        mant, ex = np.frexp(amax / 6.0)
        byte = np.where(mant > 0.5, ex, ex - 1) + 127
    byte = np.clip(np.where(amax > 0, byte, 1), 1, 254)
    scaled = (w * np.exp2(127.0 - byte)[:, None, :]).reshape(k, n).astype(np.float32)
    by_word = np.ascontiguousarray(scaled.reshape(k // 512, 128, 4, n).transpose(0, 1, 3, 2))
    if fmt == "e4m3":
        words = by_word.astype(ml_dtypes.float8_e4m3fn).view(np.uint8)
    else:
        c = by_word.astype(ml_dtypes.float4_e2m1fn).view(np.uint8) & 0xF
        words = (c[..., 0::2] | (c[..., 1::2] << 4)).reshape(k // 512, 128, 2 * n)
    return np.ascontiguousarray(words), np.ascontiguousarray(byte.astype(np.uint8).reshape(k // 512, 16, n))


def unpack_weight(words, scales, fmt):
    g, _, n = scales.shape
    words = np.ascontiguousarray(words).reshape(g, 128, n, -1)
    if fmt == "e4m3":
        vals = words.view(ml_dtypes.float8_e4m3fn).astype(np.float64)
    else:
        nib = np.empty((g, 128, n, 4), np.uint8)
        nib[..., 0::2] = words & 0xF
        nib[..., 1::2] = words >> 4
        vals = E2M1[nib]
    vals = vals * np.repeat(np.exp2(scales.astype(np.float64) - 127.0), 8, axis=1)[..., None]
    return vals.transpose(0, 1, 3, 2).reshape(g * 512, n)


def gelu(v):
    return 0.5 * v * (1.0 + np.tanh(np.sqrt(2.0 / np.pi) * (v + 0.044715 * v**3)))


def bf(x):
    return np.asarray(x, np.float32).astype(ml_dtypes.bfloat16)


def planes(Y):
    n, m = Y.shape
    b = f64(bf(Y)).reshape(n // 32, 32, m)
    amax = np.abs(b).max(1)
    byte = np.clip(np.where(amax > 0, np.frexp(amax)[1] - 1 + 127 - 7, 1), 1, 254)
    codes = (b * np.exp2(127.0 - byte)[:, None, :]).reshape(n, m).astype(np.float32).astype(ml_dtypes.float8_e4m3fn).view(np.uint8)
    words = codes.reshape(n // 512, 128, 4, m).transpose(0, 1, 3, 2)
    return np.ascontiguousarray(words), np.ascontiguousarray(byte.astype(np.uint8).reshape(n // 512, 16, m))


K, T, S, H, T2, P, N = 1024, 4096, 1024, 1024, 2048, 1024, 512


def setup_inputs():
    n = np.random.standard_normal
    s = mx_kscale(K)[:, None]
    u = mx_kscale(H)[:, None]
    size = np.exp(0.8 * n(N))
    tab_words, tab_scales = pack_weight(n((K, T)) * s, "e4m3")
    w4_words, w4_scales = pack_weight(n((H, N)) * size / np.sqrt(H) / u, "e2m1")
    return {
        "tab_words": tab_words,
        "tab_scales": tab_scales,
        "offs": striped(np.random.permutation(T)[:S]),
        "offs2": striped(np.random.permutation(T2)[:S]),
        "offs3": striped(np.random.permutation(T2)[:P]),
        "w1": (1.4 * n((K, H)) / np.sqrt(K) / s).astype(np.float32),
        "b1": (0.5 * n(H)).astype(np.float32),
        "gain": (np.random.uniform(0.8, 1.8, H) * u[:, 0]).astype(np.float32),
        "page0": (0.8 * n((H, T2)) * u).astype(np.float32),
        "w4_words": w4_words,
        "w4_scales": w4_scales,
        "traffic": (0.7 * n((N, P)) * size[:, None]).astype(np.float32),
    }


def reference(tab_words, tab_scales, offs, offs2, offs3, w1, b1, gain, page0, w4_words, w4_scales, traffic):
    v = unpack_weight(tab_words, tab_scales, "e4m3")[:, unstriped(offs)]
    w4 = unpack_weight(w4_words, w4_scales, "e2m1")
    d = (mxq(f64(w1), 0, "e4m3").T @ v) + f64(b1)[:, None]
    h = np.tanh(d) * f64(gain)[:, None]
    page = f64(page0).copy()
    l2 = unstriped(offs2)
    page[:, l2] = page[:, l2] + h
    x = page[:, unstriped(offs3)]
    y = (w4.T @ mxq(x, 0, "e4m3")) + f64(traffic)
    words, scales = planes(y)
    return y, words, scales

@@ -1,0 +1,301 @@
+from contextlib import ExitStack
+
+import concourse.mybir as mybir
+
+K, T, S, H, T2, PICK, N = 1024, 4096, 1024, 1024, 2048, 1024, 512
+FLOPS = 2 * K * H * S + 2 * H * N * PICK
+
+F32 = mybir.dt.float32
+BF16 = mybir.dt.bfloat16
+I32 = mybir.dt.int32
+U32 = mybir.dt.uint32
+U16 = mybir.dt.uint16
+U8 = mybir.dt.uint8
+FP8X4 = mybir.dt.float8_e4m3fn_x4
+FP4X4 = mybir.dt.float4_e2m1fn_x4
+ADD = mybir.AluOpType.add
+TANH = mybir.ActivationFunctionType.Tanh
+COPY = mybir.ActivationFunctionType.Copy
+
+P = 128
+PACK = 4
+PASS = P * PACK
+BANK = 512
+SLICES = H // P
+PIECE = 256
+PIECES = PICK // PIECE
+LIST_ROWS = 16
+
+
+def tile_list_pothole_segment_update_kernel(
+    tc, tab_words, tab_scales, offs, offs2, offs3, w1, b1, gain, page0, w4_words, w4_scales, traffic,
+    out_0, out_1, out_2,
+):
+    nc = tc.nc
+    with ExitStack() as ctx:
+        keep = ctx.enter_context(tc.tile_pool(name="keep", bufs=1))
+        ring = ctx.enter_context(tc.tile_pool(name="ring", bufs=2))
+        psum = ctx.enter_context(tc.psum_pool(name="psum", bufs=1))
+
+        list1 = keep.tile([P, S // LIST_ROWS], U16)
+        list2 = keep.tile([P, S // LIST_ROWS], U16)
+        list3 = keep.tile([P, PICK // LIST_ROWS], U16)
+        pages = [keep.tile([P, T2], F32, name=f"page{s}") for s in range(SLICES)]
+        tab_w = [keep.tile([P, T], I32, name=f"tab_w{a}") for a in range(2)]
+        tab_s = keep.tile([P, T], U8)
+        v_w = [keep.tile([P, S], U32, name=f"v_w{a}", align_bytes=64) for a in range(2)]
+        v_s = keep.tile([P, S], U8, align_bytes=64)
+        w1_w = [[keep.tile([P, PASS], U32, name=f"w1_w{a}{b}", align_bytes=64) for b in range(2)] for a in range(2)]
+        w1_s = [[keep.tile([P, PASS], U8, name=f"w1_s{a}{b}", align_bytes=64) for b in range(2)] for a in range(2)]
+        w4_w_raw = keep.tile([P, 2, 2 * N], U8)
+        w4_s_raw = keep.tile([P, 2, N], U8)
+        w4_w = keep.tile([P, 2, 2 * N], U8, align_bytes=64)
+        w4_s = keep.tile([P, 2, N], U8, align_bytes=64)
+        bias = keep.tile([P, SLICES], F32)
+        gains = keep.tile([P, SLICES], F32)
+        x_first = keep.tile([P, PACK, PICK], F32)
+        x_second = [keep.tile([P, PACK, PIECE], F32, name=f"x_second{c}") for c in range(PIECES)]
+        x_w = [keep.tile([P, PICK], U32, name=f"x_w{b}", align_bytes=64) for b in range(2)]
+        x_s = [keep.tile([P, PICK], U8, name=f"x_s{b}", align_bytes=64) for b in range(2)]
+        y_w = keep.tile([P, PICK], I32, align_bytes=64)
+        y_s = keep.tile([P, PICK], U8, align_bytes=64)
+        banks = [psum.tile([P, BANK], F32, name=f"bank{i}") for i in range(8)]
+
+        def load_page(s):
+            b, t = divmod(s, PACK)
+            rows = page0[b * PASS : (b + 1) * PASS, :].rearrange("(p t) c -> p t c", t=PACK)
+            nc.sync.dma_start(out=pages[s][:], in_=rows[:, t, :])
+
+        def load_w1(a, b):
+            raw = ring.tile([P, PACK, PASS], F32, name="w1_raw", tag="raw")
+            block = w1[a * PASS : (a + 1) * PASS, b * PASS : (b + 1) * PASS]
+            nc.sync.dma_start(out=raw[:], in_=block.rearrange("(p j) c -> p j c", j=PACK))
+            return raw
+
+        def quantize_w1(a, b, raw):
+            rounded = ring.tile([P, PACK * PASS], BF16, name="w1_bf", tag="wide", align_bytes=64)
+            nc.scalar.copy(
+                out=rounded[:].rearrange("p (t m j) -> p m t j", t=PACK, j=PACK),
+                in_=raw[:].rearrange("p j (m t) -> p m t j", t=PACK),
+            )
+            nc.vector.quantize_mx(out=w1_w[a][b][:].bitcast(FP8X4), scales=w1_s[a][b][:], in_=rounded[:])
+
+        def load_table(a):
+            words = tab_words[a].rearrange("p t i -> p (t i)").bitcast(I32)
+            nc.sync.dma_start(out=tab_w[a][:], in_=words)
+
+        def slot(s, c):
+            b, t = divmod(s, PACK)
+            if b == 0:
+                return x_first[:, t, c * PIECE : (c + 1) * PIECE]
+            return x_second[c][:, t, :]
+
+        def slot_runs(s):
+            if s < PACK:
+                return [(0, 2), (2, 2)]
+            return [(c, 1) for c in range(PIECES)]
+
+        def slot_run(s, c, n):
+            if s < PACK:
+                return x_first[:, s, c * PIECE : (c + n) * PIECE]
+            return x_second[c][:, s - PACK, :]
+
+        nc.vector.memset(tab_s[:].bitcast(I32), 0)
+        nc.vector.memset(w4_s_raw[:].rearrange("p a c -> p (a c)").bitcast(I32), 0)
+        for q in range(4):
+            nc.sync.dma_start(
+                out=tab_s[32 * q : 32 * q + 8, :].bitcast(I32),
+                in_=tab_scales[:, 4 * q : 4 * q + 4, :].bitcast(I32),
+            )
+
+        def load_w4_scales(q):
+            nc.sync.dma_start(
+                out=w4_s_raw[32 * q : 32 * q + 4, :, :].bitcast(I32),
+                in_=w4_scales[:, 4 * q : 4 * q + 4, :].rearrange("a r c -> r a c").bitcast(I32),
+            )
+
+        def load_vector(tile, vec):
+            nc.sync.dma_start(
+                out=tile[:].rearrange("p (b t) -> p b t", t=PACK),
+                in_=vec.rearrange("(b p t) -> p b t", p=P, t=PACK),
+            )
+
+        nc.sync.dma_start(list2[:], offs2)
+        load_page(0)
+        nc.sync.dma_start(list1[:], offs)
+        raw_first = [load_w1(0, 0)]
+        nc.sync.dma_start(out=w4_w_raw[:].bitcast(I32), in_=w4_words.rearrange("a p c -> p a c").bitcast(I32))
+        load_w4_scales(0)
+        raw_first.append(load_w1(1, 0))
+        load_w4_scales(1)
+        load_w4_scales(2)
+        load_table(0)
+        load_w4_scales(3)
+        load_vector(bias, b1)
+        load_vector(gains, gain)
+        load_table(1)
+        load_page(1)
+        nc.sync.dma_start(list3[:], offs3)
+        load_page(2)
+
+        nc.vector.tensor_copy(
+            out=w4_w[:].rearrange("p a (t m e) -> p a m t e", t=PACK, e=2),
+            in_=w4_w_raw[:].rearrange("p a (m t e) -> p a m t e", t=PACK, e=2),
+        )
+        nc.vector.tensor_copy(
+            out=w4_s[:].rearrange("p a (t m) -> p a m t", t=PACK),
+            in_=w4_s_raw[:].rearrange("p a (m t) -> p a m t", t=PACK),
+        )
+
+        olds = {}
+
+        def fetch_old(s):
+            olds[s] = ring.tile([P, S], F32, name="old", tag="old", bufs=5)
+            nc.vector.tensor_copy(out=olds[s][:], in_=pages[s][:].indirect(list2[:]))
+
+        fetch_old(0)
+        nc.vector.tensor_copy(out=v_s[:], in_=tab_s[:].indirect(list1[:]))
+        for a in range(2):
+            quantize_w1(a, 0, raw_first[a])
+        nc.vector.tensor_copy(out=v_w[0][:], in_=tab_w[0][:].bitcast(U32).indirect(list1[:]))
+        for j in range(2):
+            nc.vector.tensor_copy(
+                out=v_w[1][:, j * BANK : (j + 1) * BANK],
+                in_=tab_w[1][:].bitcast(U32).indirect(list1[:, j * 32 : (j + 1) * 32]),
+            )
+
+        raw_second = [load_w1(a, 1) for a in range(2)]
+        for s in range(3, SLICES):
+            load_page(s)
+
+        def make_h(s):
+            b, t = divmod(s, PACK)
+            cols = slice(t * P, (t + 1) * P)
+            h = ring.tile([P, S], F32, name="h", tag="h", bufs=3)
+            park = (s - 1) % SLICES
+            for j in range(2):
+                bank = banks[4 + (2 * s + j) % 4]
+                half = slice(j * BANK, (j + 1) * BANK)
+                for a in range(2):
+                    nc.tensor.matmul_mx(
+                        out=bank[:],
+                        lhsT=w1_w[a][b][:, cols].bitcast(FP8X4),
+                        lhsT_scale=w1_s[a][b][:, cols],
+                        rhs=v_w[a][:, half].bitcast(FP8X4),
+                        rhs_scale=v_s[4 * a : P, half],
+                        start=(a == 0),
+                        stop=(a == 1),
+                    )
+                for c, n in slot_runs(park):
+                    if c // 2 == j:
+                        lo = c * PIECE - j * BANK
+                        nc.scalar.activation(
+                            out=slot_run(park, c, n), in_=bank[:, lo : lo + n * PIECE], func=TANH,
+                            bias=bias[:, s : s + 1],
+                        )
+                for c, n in slot_runs(park):
+                    if c // 2 == j:
+                        nc.scalar.activation(
+                            out=h[:, c * PIECE : (c + n) * PIECE], in_=slot_run(park, c, n), func=COPY,
+                            scale=gains[:, s : s + 1],
+                        )
+            return h
+
+        def put_new(s, h):
+            nc.vector.tensor_tensor(out=pages[s][:].indirect(list2[:]), in0=olds[s][:], in1=h[:], op=ADD)
+
+        def fetch_x(s, c):
+            cols = PIECE // LIST_ROWS
+            nc.vector.tensor_copy(out=slot(s, c), in_=pages[s][:].indirect(list3[:, c * cols : (c + 1) * cols]))
+
+        def round_interleaved(engine_copy, out, in_):
+            engine_copy(
+                out=out.rearrange("p (c i t) -> p c t i", i=4, t=PACK),
+                in_=in_.rearrange("p t (c i) -> p c t i", i=4),
+            )
+
+        for s in range(SLICES):
+            if s == 2:
+                for a in range(2):
+                    quantize_w1(a, 1, raw_second[a])
+            h = make_h(s)
+            if s + 1 < SLICES:
+                fetch_old(s + 1)
+            put_new(s, h)
+            if 1 <= s <= PACK:
+                nc.vector.tensor_copy(out=x_first[:, s - 1, :], in_=pages[s - 1][:].indirect(list3[:]))
+            elif PACK < s < SLICES - 1:
+                for c in range(PIECES):
+                    fetch_x(s - 1, c)
+
+        ys = []
+        rows = traffic.rearrange("(p t) m -> p t m", t=PACK)
+        for half in range(2):
+            pair = ring.tile([P, 2, PACK, PIECE], F32, name="y_pair", tag="raw")
+            for c in range(2):
+                m0 = (2 * half + c) * PIECE
+                nc.sync.dma_start(out=pair[:, c, :, :], in_=rows[:, :, m0 : m0 + PIECE])
+                ys.append(pair[:, c, :, :])
+
+        def second_product(b, c):
+            cols = slice(c * PIECE, (c + 1) * PIECE)
+            for t in range(PACK):
+                bank = banks[2 * c + t // 2]
+                nc.tensor.matmul_mx(
+                    out=bank[:, (t % 2) * PIECE : (t % 2 + 1) * PIECE],
+                    lhsT=w4_w[:, b, 2 * P * t : 2 * P * (t + 1)].bitcast(FP4X4),
+                    lhsT_scale=w4_s[:, b, P * t : P * (t + 1)],
+                    rhs=x_w[b][:, cols].bitcast(FP8X4),
+                    rhs_scale=x_s[b][:, cols],
+                    start=(b == 0 and t % 2 == 0),
+                    stop=(b == 1 and t % 2 == 1),
+                )
+
+        for half in range(2):
+            cols = slice(half * BANK, (half + 1) * BANK)
+            rounded = ring.tile([P, PACK * BANK], BF16, name="x_bf_wide", tag="wide", align_bytes=64)
+            round_interleaved(nc.scalar.copy, rounded[:], x_first[:, :, cols])
+            nc.vector.quantize_mx(out=x_w[0][:, cols].bitcast(FP8X4), scales=x_s[0][:, cols], in_=rounded[:])
+        for c in range(PIECES):
+            second_product(0, c)
+
+        for c in range(PIECES):
+            fetch_x(SLICES - 2, c)
+            fetch_x(SLICES - 1, c)
+
+        out_rows = out_0.rearrange("(p t) m -> p t m", t=PACK)
+        out_words = out_1[0].rearrange("p m t -> p (m t)").bitcast(I32)
+
+        def quantize_x(c):
+            cols = slice(c * PIECE, (c + 1) * PIECE)
+            rounded = ring.tile([P, PACK * PIECE], BF16, name="x_bf", tag="narrow", bufs=4, align_bytes=64)
+            round_interleaved(nc.scalar.copy, rounded[:], x_second[c][:])
+            nc.vector.quantize_mx(out=x_w[1][:, cols].bitcast(FP8X4), scales=x_s[1][:, cols], in_=rounded[:])
+            second_product(1, c)
+
+        def add_traffic(c):
+            cols = slice(c * PIECE, (c + 1) * PIECE)
+            for u in range(2):
+                part = ys[c][:, 2 * u : 2 * u + 2, :].rearrange("p t m -> p (t m)")
+                nc.vector.tensor_tensor(out=part, in0=banks[2 * c + u][:], in1=part, op=ADD)
+            nc.sync.dma_start(out=out_rows[:, :, cols], in_=ys[c])
+
+        def quantize_y(c):
+            cols = slice(c * PIECE, (c + 1) * PIECE)
+            rounded = ring.tile([P, PACK * PIECE], BF16, name="y_bf", tag="narrow", bufs=4, align_bytes=64)
+            copy = nc.vector.tensor_copy if c == PIECES - 1 else nc.scalar.copy
+            round_interleaved(copy, rounded[:], ys[c])
+            nc.vector.quantize_mx(out=y_w[:, cols].bitcast(FP8X4), scales=y_s[:, cols], in_=rounded[:])
+            nc.sync.dma_start(out=out_words[:, cols], in_=y_w[:, cols])
+
+        for c in range(PIECES):
+            quantize_x(c)
+        for c in range(PIECES):
+            add_traffic(c)
+            quantize_y(c)
+        for q in range(4):
+            queue = nc.scalar if q % 2 else nc.sync
+            queue.dma_start(
+                out=out_2[0, 4 * q : 4 * q + 4, :].bitcast(I32),
+                in_=y_s[32 * q : 32 * q + 4, :].bitcast(I32),
+            )

@@ -20,11 +20,19 @@ COPY = mybir.ActivationFunctionType.Copy
 P = 128
 PACK = 4
 PASS = P * PACK
+PASSES = 2
+QUADRANTS = 4
+QUADRANT = P // QUADRANTS
+SCALE_ROWS = 4
 BANK = 512
+BANKS = 8
+HALVES = S // BANK
 SLICES = H // P
+PER_COLUMN = 16
+LINE = 4
 PIECE = 256
 PIECES = PICK // PIECE
-LIST_ROWS = 16
+EARLY_PAGES = 6
 
 
 def tile_list_pothole_segment_update_kernel(
@@ -37,29 +45,35 @@ def tile_list_pothole_segment_update_kernel(
         ring = ctx.enter_context(tc.tile_pool(name="ring", bufs=2))
         psum = ctx.enter_context(tc.psum_pool(name="psum", bufs=1))
 
-        list1 = keep.tile([P, S // LIST_ROWS], U16)
-        list2 = keep.tile([P, S // LIST_ROWS], U16)
-        list3 = keep.tile([P, PICK // LIST_ROWS], U16)
+        list1 = keep.tile([P, S // PER_COLUMN], U16)
+        list2 = keep.tile([P, S // PER_COLUMN], U16)
+        list3 = keep.tile([P, PICK // PER_COLUMN], U16)
         pages = [keep.tile([P, T2], F32, name=f"page{s}") for s in range(SLICES)]
-        tab_w = [keep.tile([P, T], I32, name=f"tab_w{a}") for a in range(2)]
+        tab_w = [keep.tile([P, T], I32, name=f"tab_w{a}") for a in range(PASSES)]
         tab_s = keep.tile([P, T], U8)
-        v_w = [keep.tile([P, S], U32, name=f"v_w{a}", align_bytes=64) for a in range(2)]
+        v_w = [keep.tile([P, S], U32, name=f"v_w{a}", align_bytes=64) for a in range(PASSES)]
         v_s = keep.tile([P, S], U8, align_bytes=64)
-        w1_w = [[keep.tile([P, PASS], U32, name=f"w1_w{a}{b}", align_bytes=64) for b in range(2)] for a in range(2)]
-        w1_s = [[keep.tile([P, PASS], U8, name=f"w1_s{a}{b}", align_bytes=64) for b in range(2)] for a in range(2)]
-        w4_w_raw = keep.tile([P, 2, 2 * N], U8)
-        w4_s_raw = keep.tile([P, 2, N], U8)
-        w4_w = keep.tile([P, 2, 2 * N], U8, align_bytes=64)
-        w4_s = keep.tile([P, 2, N], U8, align_bytes=64)
+        w1_w = [
+            [keep.tile([P, PASS], U32, name=f"w1_w{a}{b}", align_bytes=64) for b in range(PASSES)]
+            for a in range(PASSES)
+        ]
+        w1_s = [
+            [keep.tile([P, PASS], U8, name=f"w1_s{a}{b}", align_bytes=64) for b in range(PASSES)]
+            for a in range(PASSES)
+        ]
+        w4_w_raw = keep.tile([P, PASSES, 2 * N], U8)
+        w4_s_raw = keep.tile([P, PASSES, N], U8)
+        w4_w = keep.tile([P, PASSES, 2 * N], U8, align_bytes=64)
+        w4_s = keep.tile([P, PASSES, N], U8, align_bytes=64)
         bias = keep.tile([P, SLICES], F32)
         gains = keep.tile([P, SLICES], F32)
         x_first = keep.tile([P, PACK, PICK], F32)
-        x_second = [keep.tile([P, PACK, PIECE], F32, name=f"x_second{c}") for c in range(PIECES)]
-        x_w = [keep.tile([P, PICK], U32, name=f"x_w{b}", align_bytes=64) for b in range(2)]
-        x_s = [keep.tile([P, PICK], U8, name=f"x_s{b}", align_bytes=64) for b in range(2)]
+        x_piece = [keep.tile([P, PACK, PIECE], F32, name=f"x_piece{i}") for i in range(2)]
+        x_w = [keep.tile([P, PICK], U32, name=f"x_w{b}", align_bytes=64) for b in range(PASSES)]
+        x_s = [keep.tile([P, PICK], U8, name=f"x_s{b}", align_bytes=64) for b in range(PASSES)]
         y_w = keep.tile([P, PICK], I32, align_bytes=64)
         y_s = keep.tile([P, PICK], U8, align_bytes=64)
-        banks = [psum.tile([P, BANK], F32, name=f"bank{i}") for i in range(8)]
+        banks = [psum.tile([P, BANK], F32, name=f"bank{i}") for i in range(BANKS)]
 
         def load_page(s):
             b, t = divmod(s, PACK)
@@ -84,34 +98,29 @@ def tile_list_pothole_segment_update_kernel(
             words = tab_words[a].rearrange("p t i -> p (t i)").bitcast(I32)
             nc.sync.dma_start(out=tab_w[a][:], in_=words)
 
-        def slot(s, c):
-            b, t = divmod(s, PACK)
-            if b == 0:
-                return x_first[:, t, c * PIECE : (c + 1) * PIECE]
-            return x_second[c][:, t, :]
-
-        def slot_runs(s):
-            if s < PACK:
-                return [(0, 2), (2, 2)]
-            return [(c, 1) for c in range(PIECES)]
-
-        def slot_run(s, c, n):
-            if s < PACK:
-                return x_first[:, s, c * PIECE : (c + n) * PIECE]
-            return x_second[c][:, s - PACK, :]
+        def parking(s):
+            if s in (0, SLICES - 1):
+                return [x_piece[j][:, :, 0 : BANK // PACK] for j in range(HALVES)]
+            if s <= PACK:
+                row = x_first[:, s - 1, :]
+            else:
+                tile = ring.tile([P, S], F32, name="parked", tag="wide", align_bytes=64)
+                row = tile[:]
+            return [row[:, j * BANK : (j + 1) * BANK].rearrange("p (t m) -> p t m", t=PACK) for j in range(HALVES)]
 
         nc.vector.memset(tab_s[:].bitcast(I32), 0)
         nc.vector.memset(w4_s_raw[:].rearrange("p a c -> p (a c)").bitcast(I32), 0)
-        for q in range(4):
+
+        def load_table_scales(q):
             nc.sync.dma_start(
-                out=tab_s[32 * q : 32 * q + 8, :].bitcast(I32),
-                in_=tab_scales[:, 4 * q : 4 * q + 4, :].bitcast(I32),
+                out=tab_s[QUADRANT * q : QUADRANT * q + PASSES * SCALE_ROWS, :].bitcast(I32),
+                in_=tab_scales[:, SCALE_ROWS * q : SCALE_ROWS * (q + 1), :].bitcast(I32),
             )
 
         def load_w4_scales(q):
             nc.sync.dma_start(
-                out=w4_s_raw[32 * q : 32 * q + 4, :, :].bitcast(I32),
-                in_=w4_scales[:, 4 * q : 4 * q + 4, :].rearrange("a r c -> r a c").bitcast(I32),
+                out=w4_s_raw[QUADRANT * q : QUADRANT * q + SCALE_ROWS, :, :].bitcast(I32),
+                in_=w4_scales[:, SCALE_ROWS * q : SCALE_ROWS * (q + 1), :].rearrange("a r c -> r a c").bitcast(I32),
             )
 
         def load_vector(tile, vec):
@@ -123,119 +132,122 @@ def tile_list_pothole_segment_update_kernel(
         nc.sync.dma_start(list2[:], offs2)
         load_page(0)
         nc.sync.dma_start(list1[:], offs)
-        raw_first = [load_w1(0, 0)]
-        nc.sync.dma_start(out=w4_w_raw[:].bitcast(I32), in_=w4_words.rearrange("a p c -> p a c").bitcast(I32))
-        load_w4_scales(0)
-        raw_first.append(load_w1(1, 0))
-        load_w4_scales(1)
-        load_w4_scales(2)
-        load_table(0)
-        load_w4_scales(3)
-        load_vector(bias, b1)
-        load_vector(gains, gain)
-        load_table(1)
         load_page(1)
         nc.sync.dma_start(list3[:], offs3)
+        load_vector(bias, b1)
+        load_vector(gains, gain)
         load_page(2)
+        nc.sync.dma_start(out=w4_w_raw[:].bitcast(I32), in_=w4_words.rearrange("a p c -> p a c").bitcast(I32))
+        load_page(3)
+        for q in range(QUADRANTS):
+            load_table_scales(q)
+        load_page(4)
+        raw_first = [load_w1(0, 0)]
+        load_page(5)
+        raw_first.append(load_w1(1, 0))
+        load_table(0)
+        for q in range(QUADRANTS):
+            load_w4_scales(q)
+        load_table(1)
+        for s in range(EARLY_PAGES, SLICES):
+            load_page(s)
 
         nc.vector.tensor_copy(
-            out=w4_w[:].rearrange("p a (t m e) -> p a m t e", t=PACK, e=2),
-            in_=w4_w_raw[:].rearrange("p a (m t e) -> p a m t e", t=PACK, e=2),
+            out=w4_w[:].rearrange("p a (t m e) -> p a t m e", t=PACK, e=2),
+            in_=w4_w_raw[:].rearrange("p a (m t e) -> p a t m e", t=PACK, e=2),
         )
         nc.vector.tensor_copy(
-            out=w4_s[:].rearrange("p a (t m) -> p a m t", t=PACK),
-            in_=w4_s_raw[:].rearrange("p a (m t) -> p a m t", t=PACK),
+            out=w4_s[:].rearrange("p a (t m) -> p a t m", t=PACK),
+            in_=w4_s_raw[:].rearrange("p a (m t) -> p a t m", t=PACK),
         )
 
         olds = {}
 
         def fetch_old(s):
-            olds[s] = ring.tile([P, S], F32, name="old", tag="old", bufs=5)
+            olds[s] = ring.tile([P, S], F32, name="old", tag="old", bufs=SLICES)
             nc.vector.tensor_copy(out=olds[s][:], in_=pages[s][:].indirect(list2[:]))
 
-        fetch_old(0)
+        for s in range(EARLY_PAGES):
+            fetch_old(s)
         nc.vector.tensor_copy(out=v_s[:], in_=tab_s[:].indirect(list1[:]))
-        for a in range(2):
+        for a in range(PASSES):
             quantize_w1(a, 0, raw_first[a])
         nc.vector.tensor_copy(out=v_w[0][:], in_=tab_w[0][:].bitcast(U32).indirect(list1[:]))
-        for j in range(2):
+        half_columns = BANK // PER_COLUMN
+        for j in range(HALVES):
             nc.vector.tensor_copy(
                 out=v_w[1][:, j * BANK : (j + 1) * BANK],
-                in_=tab_w[1][:].bitcast(U32).indirect(list1[:, j * 32 : (j + 1) * 32]),
+                in_=tab_w[1][:].bitcast(U32).indirect(list1[:, j * half_columns : (j + 1) * half_columns]),
             )
 
-        raw_second = [load_w1(a, 1) for a in range(2)]
-        for s in range(3, SLICES):
-            load_page(s)
+        raw_second = [load_w1(a, 1) for a in range(PASSES)]
 
         def make_h(s):
             b, t = divmod(s, PACK)
             cols = slice(t * P, (t + 1) * P)
             h = ring.tile([P, S], F32, name="h", tag="h", bufs=3)
-            park = (s - 1) % SLICES
-            for j in range(2):
-                bank = banks[4 + (2 * s + j) % 4]
+            parked = parking(s)
+            for j in range(HALVES):
+                bank = banks[BANKS // 2 + (HALVES * s + j) % (BANKS // 2)]
                 half = slice(j * BANK, (j + 1) * BANK)
-                for a in range(2):
+                for a in range(PASSES):
                     nc.tensor.matmul_mx(
                         out=bank[:],
                         lhsT=w1_w[a][b][:, cols].bitcast(FP8X4),
                         lhsT_scale=w1_s[a][b][:, cols],
                         rhs=v_w[a][:, half].bitcast(FP8X4),
-                        rhs_scale=v_s[4 * a : P, half],
+                        rhs_scale=v_s[SCALE_ROWS * a : P, half],
                         start=(a == 0),
-                        stop=(a == 1),
+                        stop=(a == PASSES - 1),
                     )
-                for c, n in slot_runs(park):
-                    if c // 2 == j:
-                        lo = c * PIECE - j * BANK
-                        nc.scalar.activation(
-                            out=slot_run(park, c, n), in_=bank[:, lo : lo + n * PIECE], func=TANH,
-                            bias=bias[:, s : s + 1],
-                        )
-                for c, n in slot_runs(park):
-                    if c // 2 == j:
-                        nc.scalar.activation(
-                            out=h[:, c * PIECE : (c + n) * PIECE], in_=slot_run(park, c, n), func=COPY,
-                            scale=gains[:, s : s + 1],
-                        )
+                nc.scalar.activation(
+                    out=parked[j], in_=bank[:].rearrange("p (t m) -> p t m", t=PACK), func=TANH,
+                    bias=bias[:, s : s + 1],
+                )
+                nc.scalar.activation(
+                    out=h[:, half].rearrange("p (t m) -> p t m", t=PACK), in_=parked[j], func=COPY,
+                    scale=gains[:, s : s + 1],
+                )
             return h
 
         def put_new(s, h):
-            nc.vector.tensor_tensor(out=pages[s][:].indirect(list2[:]), in0=olds[s][:], in1=h[:], op=ADD)
+            parts = HALVES if s == 0 else 1
+            for j in range(parts):
+                cols = slice(j * S // parts, (j + 1) * S // parts)
+                entries = list2[:, j * S // parts // PER_COLUMN : (j + 1) * S // parts // PER_COLUMN]
+                nc.vector.tensor_tensor(out=pages[s][:].indirect(entries), in0=olds[s][:, cols], in1=h[:, cols], op=ADD)
 
-        def fetch_x(s, c):
-            cols = PIECE // LIST_ROWS
-            nc.vector.tensor_copy(out=slot(s, c), in_=pages[s][:].indirect(list3[:, c * cols : (c + 1) * cols]))
+        def fetch_x(c):
+            piece_columns = PIECE // PER_COLUMN
+            for t in range(PACK):
+                window = pages[PACK + t][:].indirect(list3[:, c * piece_columns : (c + 1) * piece_columns])
+                nc.vector.tensor_copy(out=x_piece[c % 2][:, t, :], in_=window)
 
         def round_interleaved(engine_copy, out, in_):
             engine_copy(
-                out=out.rearrange("p (c i t) -> p c t i", i=4, t=PACK),
-                in_=in_.rearrange("p t (c i) -> p c t i", i=4),
+                out=out.rearrange("p (c i t) -> p c t i", i=LINE, t=PACK),
+                in_=in_.rearrange("p t (c i) -> p c t i", i=LINE),
             )
 
         for s in range(SLICES):
-            if s == 2:
-                for a in range(2):
+            if s == PACK - 2:
+                for a in range(PASSES):
                     quantize_w1(a, 1, raw_second[a])
             h = make_h(s)
-            if s + 1 < SLICES:
-                fetch_old(s + 1)
+            if s + EARLY_PAGES < SLICES:
+                fetch_old(s + EARLY_PAGES)
             put_new(s, h)
             if 1 <= s <= PACK:
                 nc.vector.tensor_copy(out=x_first[:, s - 1, :], in_=pages[s - 1][:].indirect(list3[:]))
-            elif PACK < s < SLICES - 1:
-                for c in range(PIECES):
-                    fetch_x(s - 1, c)
 
         ys = []
-        rows = traffic.rearrange("(p t) m -> p t m", t=PACK)
-        for half in range(2):
+        traffic_rows = traffic.rearrange("(p t) m -> p t m", t=PACK)
+        for pair_index in range(PIECES // 2):
             pair = ring.tile([P, 2, PACK, PIECE], F32, name="y_pair", tag="raw")
-            for c in range(2):
-                m0 = (2 * half + c) * PIECE
-                nc.sync.dma_start(out=pair[:, c, :, :], in_=rows[:, :, m0 : m0 + PIECE])
-                ys.append(pair[:, c, :, :])
+            for i in range(2):
+                m0 = (2 * pair_index + i) * PIECE
+                nc.sync.dma_start(out=pair[:, i, :, :], in_=traffic_rows[:, :, m0 : m0 + PIECE])
+                ys.append(pair[:, i, :, :])
 
         def second_product(b, c):
             cols = slice(c * PIECE, (c + 1) * PIECE)
@@ -248,28 +260,24 @@ def tile_list_pothole_segment_update_kernel(
                     rhs=x_w[b][:, cols].bitcast(FP8X4),
                     rhs_scale=x_s[b][:, cols],
                     start=(b == 0 and t % 2 == 0),
-                    stop=(b == 1 and t % 2 == 1),
+                    stop=(b == PASSES - 1 and t % 2 == 1),
                 )
 
-        for half in range(2):
-            cols = slice(half * BANK, (half + 1) * BANK)
+        for j in range(HALVES):
+            cols = slice(j * BANK, (j + 1) * BANK)
             rounded = ring.tile([P, PACK * BANK], BF16, name="x_bf_wide", tag="wide", align_bytes=64)
             round_interleaved(nc.scalar.copy, rounded[:], x_first[:, :, cols])
             nc.vector.quantize_mx(out=x_w[0][:, cols].bitcast(FP8X4), scales=x_s[0][:, cols], in_=rounded[:])
         for c in range(PIECES):
             second_product(0, c)
 
-        for c in range(PIECES):
-            fetch_x(SLICES - 2, c)
-            fetch_x(SLICES - 1, c)
-
         out_rows = out_0.rearrange("(p t) m -> p t m", t=PACK)
         out_words = out_1[0].rearrange("p m t -> p (m t)").bitcast(I32)
 
         def quantize_x(c):
             cols = slice(c * PIECE, (c + 1) * PIECE)
-            rounded = ring.tile([P, PACK * PIECE], BF16, name="x_bf", tag="narrow", bufs=4, align_bytes=64)
-            round_interleaved(nc.scalar.copy, rounded[:], x_second[c][:])
+            rounded = ring.tile([P, PACK * PIECE], BF16, name="x_bf", tag="narrow", bufs=3, align_bytes=64)
+            round_interleaved(nc.scalar.copy, rounded[:], x_piece[c % 2][:])
             nc.vector.quantize_mx(out=x_w[1][:, cols].bitcast(FP8X4), scales=x_s[1][:, cols], in_=rounded[:])
             second_product(1, c)
 
@@ -282,20 +290,26 @@ def tile_list_pothole_segment_update_kernel(
 
         def quantize_y(c):
             cols = slice(c * PIECE, (c + 1) * PIECE)
-            rounded = ring.tile([P, PACK * PIECE], BF16, name="y_bf", tag="narrow", bufs=4, align_bytes=64)
-            copy = nc.vector.tensor_copy if c == PIECES - 1 else nc.scalar.copy
-            round_interleaved(copy, rounded[:], ys[c])
+            rounded = ring.tile([P, PACK * PIECE], BF16, name="y_bf", tag="narrow", bufs=3, align_bytes=64)
+            engine_copy = nc.vector.tensor_copy if c == PIECES - 1 else nc.scalar.copy
+            round_interleaved(engine_copy, rounded[:], ys[c])
             nc.vector.quantize_mx(out=y_w[:, cols].bitcast(FP8X4), scales=y_s[:, cols], in_=rounded[:])
             nc.sync.dma_start(out=out_words[:, cols], in_=y_w[:, cols])
 
-        for c in range(PIECES):
-            quantize_x(c)
-        for c in range(PIECES):
-            add_traffic(c)
-            quantize_y(c)
-        for q in range(4):
+        fetch_x(0)
+        for c in range(PIECES + 2):
+            if c + 1 < PIECES:
+                fetch_x(c + 1)
+            if c < PIECES:
+                quantize_x(c)
+            if c >= 2:
+                quantize_y(c - 2)
+            if 1 <= c <= PIECES:
+                add_traffic(c - 1)
+
+        for q in range(QUADRANTS):
             queue = nc.scalar if q % 2 else nc.sync
             queue.dma_start(
-                out=out_2[0, 4 * q : 4 * q + 4, :].bitcast(I32),
-                in_=y_s[32 * q : 32 * q + 4, :].bitcast(I32),
+                out=out_2[0, SCALE_ROWS * q : SCALE_ROWS * (q + 1), :].bitcast(I32),
+                in_=y_s[QUADRANT * q : QUADRANT * q + SCALE_ROWS, :].bitcast(I32),
             )

from contextlib import ExitStack

import concourse.mybir as mybir

K, T, S, H, T2, PICK, N = 1024, 4096, 1024, 1024, 2048, 1024, 512
FLOPS = 2 * K * H * S + 2 * H * N * PICK

F32 = mybir.dt.float32
BF16 = mybir.dt.bfloat16
I32 = mybir.dt.int32
U32 = mybir.dt.uint32
U16 = mybir.dt.uint16
U8 = mybir.dt.uint8
FP8X4 = mybir.dt.float8_e4m3fn_x4
FP4X4 = mybir.dt.float4_e2m1fn_x4
ADD = mybir.AluOpType.add
TANH = mybir.ActivationFunctionType.Tanh
COPY = mybir.ActivationFunctionType.Copy

P = 128
PACK = 4
PASS = P * PACK
PASSES = 2
QUADRANTS = 4
QUADRANT = P // QUADRANTS
SCALE_ROWS = 4
BANK = 512
BANKS = 8
HALVES = S // BANK
SLICES = H // P
PER_COLUMN = 16
LINE = 4
PIECE = 256
PIECES = PICK // PIECE
EARLY_PAGES = 6


def tile_list_pothole_segment_update_kernel(
    tc, tab_words, tab_scales, offs, offs2, offs3, w1, b1, gain, page0, w4_words, w4_scales, traffic,
    out_0, out_1, out_2,
):
    nc = tc.nc
    with ExitStack() as ctx:
        keep = ctx.enter_context(tc.tile_pool(name="keep", bufs=1))
        ring = ctx.enter_context(tc.tile_pool(name="ring", bufs=2))
        psum = ctx.enter_context(tc.psum_pool(name="psum", bufs=1))

        list1 = keep.tile([P, S // PER_COLUMN], U16)
        list2 = keep.tile([P, S // PER_COLUMN], U16)
        list3 = keep.tile([P, PICK // PER_COLUMN], U16)
        pages = [keep.tile([P, T2], F32, name=f"page{s}") for s in range(SLICES)]
        tab_w = [keep.tile([P, T], I32, name=f"tab_w{a}") for a in range(PASSES)]
        tab_s = keep.tile([P, T], U8)
        v_w = [keep.tile([P, S], U32, name=f"v_w{a}", align_bytes=64) for a in range(PASSES)]
        v_s = keep.tile([P, S], U8, align_bytes=64)
        w1_w = [
            [keep.tile([P, PASS], U32, name=f"w1_w{a}{b}", align_bytes=64) for b in range(PASSES)]
            for a in range(PASSES)
        ]
        w1_s = [
            [keep.tile([P, PASS], U8, name=f"w1_s{a}{b}", align_bytes=64) for b in range(PASSES)]
            for a in range(PASSES)
        ]
        w4_w_raw = keep.tile([P, PASSES, 2 * N], U8)
        w4_s_raw = keep.tile([P, PASSES, N], U8)
        w4_w = keep.tile([P, PASSES, 2 * N], U8, align_bytes=64)
        w4_s = keep.tile([P, PASSES, N], U8, align_bytes=64)
        bias = keep.tile([P, SLICES], F32)
        gains = keep.tile([P, SLICES], F32)
        x_first = keep.tile([P, PACK, PICK], F32)
        x_piece = [keep.tile([P, PACK, PIECE], F32, name=f"x_piece{i}") for i in range(2)]
        x_w = [keep.tile([P, PICK], U32, name=f"x_w{b}", align_bytes=64) for b in range(PASSES)]
        x_s = [keep.tile([P, PICK], U8, name=f"x_s{b}", align_bytes=64) for b in range(PASSES)]
        y_w = keep.tile([P, PICK], I32, align_bytes=64)
        y_s = keep.tile([P, PICK], U8, align_bytes=64)
        banks = [psum.tile([P, BANK], F32, name=f"bank{i}") for i in range(BANKS)]

        def load_page(s):
            b, t = divmod(s, PACK)
            rows = page0[b * PASS : (b + 1) * PASS, :].rearrange("(p t) c -> p t c", t=PACK)
            nc.sync.dma_start(out=pages[s][:], in_=rows[:, t, :])

        def load_w1(a, b):
            raw = ring.tile([P, PACK, PASS], F32, name="w1_raw", tag="raw")
            block = w1[a * PASS : (a + 1) * PASS, b * PASS : (b + 1) * PASS]
            nc.sync.dma_start(out=raw[:], in_=block.rearrange("(p j) c -> p j c", j=PACK))
            return raw

        def quantize_w1(a, b, raw):
            rounded = ring.tile([P, PACK * PASS], BF16, name="w1_bf", tag="wide", align_bytes=64)
            nc.scalar.copy(
                out=rounded[:].rearrange("p (t m j) -> p m t j", t=PACK, j=PACK),
                in_=raw[:].rearrange("p j (m t) -> p m t j", t=PACK),
            )
            nc.vector.quantize_mx(out=w1_w[a][b][:].bitcast(FP8X4), scales=w1_s[a][b][:], in_=rounded[:])

        def load_table(a):
            words = tab_words[a].rearrange("p t i -> p (t i)").bitcast(I32)
            nc.sync.dma_start(out=tab_w[a][:], in_=words)

        def parking(s):
            if s in (0, SLICES - 1):
                return [x_piece[j][:, :, 0 : BANK // PACK] for j in range(HALVES)]
            if s <= PACK:
                row = x_first[:, s - 1, :]
            else:
                tile = ring.tile([P, S], F32, name="parked", tag="wide", align_bytes=64)
                row = tile[:]
            return [row[:, j * BANK : (j + 1) * BANK].rearrange("p (t m) -> p t m", t=PACK) for j in range(HALVES)]

        nc.vector.memset(tab_s[:].bitcast(I32), 0)
        nc.vector.memset(w4_s_raw[:].rearrange("p a c -> p (a c)").bitcast(I32), 0)

        def load_table_scales(q):
            nc.sync.dma_start(
                out=tab_s[QUADRANT * q : QUADRANT * q + PASSES * SCALE_ROWS, :].bitcast(I32),
                in_=tab_scales[:, SCALE_ROWS * q : SCALE_ROWS * (q + 1), :].bitcast(I32),
            )

        def load_w4_scales(q):
            nc.sync.dma_start(
                out=w4_s_raw[QUADRANT * q : QUADRANT * q + SCALE_ROWS, :, :].bitcast(I32),
                in_=w4_scales[:, SCALE_ROWS * q : SCALE_ROWS * (q + 1), :].rearrange("a r c -> r a c").bitcast(I32),
            )

        def load_vector(tile, vec):
            nc.sync.dma_start(
                out=tile[:].rearrange("p (b t) -> p b t", t=PACK),
                in_=vec.rearrange("(b p t) -> p b t", p=P, t=PACK),
            )

        nc.sync.dma_start(list2[:], offs2)
        load_page(0)
        nc.sync.dma_start(list1[:], offs)
        load_page(1)
        nc.sync.dma_start(list3[:], offs3)
        load_vector(bias, b1)
        load_vector(gains, gain)
        load_page(2)
        nc.sync.dma_start(out=w4_w_raw[:].bitcast(I32), in_=w4_words.rearrange("a p c -> p a c").bitcast(I32))
        load_page(3)
        for q in range(QUADRANTS):
            load_table_scales(q)
        load_page(4)
        raw_first = [load_w1(0, 0)]
        load_page(5)
        raw_first.append(load_w1(1, 0))
        load_table(0)
        for q in range(QUADRANTS):
            load_w4_scales(q)
        load_table(1)
        for s in range(EARLY_PAGES, SLICES):
            load_page(s)

        nc.vector.tensor_copy(
            out=w4_w[:].rearrange("p a (t m e) -> p a t m e", t=PACK, e=2),
            in_=w4_w_raw[:].rearrange("p a (m t e) -> p a t m e", t=PACK, e=2),
        )
        nc.vector.tensor_copy(
            out=w4_s[:].rearrange("p a (t m) -> p a t m", t=PACK),
            in_=w4_s_raw[:].rearrange("p a (m t) -> p a t m", t=PACK),
        )

        olds = {}

        def fetch_old(s):
            olds[s] = ring.tile([P, S], F32, name="old", tag="old", bufs=SLICES)
            nc.vector.tensor_copy(out=olds[s][:], in_=pages[s][:].indirect(list2[:]))

        for s in range(EARLY_PAGES):
            fetch_old(s)
        nc.vector.tensor_copy(out=v_s[:], in_=tab_s[:].indirect(list1[:]))
        for a in range(PASSES):
            quantize_w1(a, 0, raw_first[a])
        nc.vector.tensor_copy(out=v_w[0][:], in_=tab_w[0][:].bitcast(U32).indirect(list1[:]))
        half_columns = BANK // PER_COLUMN
        for j in range(HALVES):
            nc.vector.tensor_copy(
                out=v_w[1][:, j * BANK : (j + 1) * BANK],
                in_=tab_w[1][:].bitcast(U32).indirect(list1[:, j * half_columns : (j + 1) * half_columns]),
            )

        raw_second = [load_w1(a, 1) for a in range(PASSES)]

        def make_h(s):
            b, t = divmod(s, PACK)
            cols = slice(t * P, (t + 1) * P)
            h = ring.tile([P, S], F32, name="h", tag="h", bufs=3)
            parked = parking(s)
            for j in range(HALVES):
                bank = banks[BANKS // 2 + (HALVES * s + j) % (BANKS // 2)]
                half = slice(j * BANK, (j + 1) * BANK)
                for a in range(PASSES):
                    nc.tensor.matmul_mx(
                        out=bank[:],
                        lhsT=w1_w[a][b][:, cols].bitcast(FP8X4),
                        lhsT_scale=w1_s[a][b][:, cols],
                        rhs=v_w[a][:, half].bitcast(FP8X4),
                        rhs_scale=v_s[SCALE_ROWS * a : P, half],
                        start=(a == 0),
                        stop=(a == PASSES - 1),
                    )
                nc.scalar.activation(
                    out=parked[j], in_=bank[:].rearrange("p (t m) -> p t m", t=PACK), func=TANH,
                    bias=bias[:, s : s + 1],
                )
                nc.scalar.activation(
                    out=h[:, half].rearrange("p (t m) -> p t m", t=PACK), in_=parked[j], func=COPY,
                    scale=gains[:, s : s + 1],
                )
            return h

        def put_new(s, h):
            parts = HALVES if s == 0 else 1
            for j in range(parts):
                cols = slice(j * S // parts, (j + 1) * S // parts)
                entries = list2[:, j * S // parts // PER_COLUMN : (j + 1) * S // parts // PER_COLUMN]
                nc.vector.tensor_tensor(out=pages[s][:].indirect(entries), in0=olds[s][:, cols], in1=h[:, cols], op=ADD)

        def fetch_x(c):
            piece_columns = PIECE // PER_COLUMN
            for t in range(PACK):
                window = pages[PACK + t][:].indirect(list3[:, c * piece_columns : (c + 1) * piece_columns])
                nc.vector.tensor_copy(out=x_piece[c % 2][:, t, :], in_=window)

        def round_interleaved(engine_copy, out, in_):
            engine_copy(
                out=out.rearrange("p (c i t) -> p c t i", i=LINE, t=PACK),
                in_=in_.rearrange("p t (c i) -> p c t i", i=LINE),
            )

        for s in range(SLICES):
            if s == PACK - 2:
                for a in range(PASSES):
                    quantize_w1(a, 1, raw_second[a])
            h = make_h(s)
            if s + EARLY_PAGES < SLICES:
                fetch_old(s + EARLY_PAGES)
            put_new(s, h)
            if 1 <= s <= PACK:
                nc.vector.tensor_copy(out=x_first[:, s - 1, :], in_=pages[s - 1][:].indirect(list3[:]))

        ys = []
        traffic_rows = traffic.rearrange("(p t) m -> p t m", t=PACK)
        for pair_index in range(PIECES // 2):
            pair = ring.tile([P, 2, PACK, PIECE], F32, name="y_pair", tag="raw")
            for i in range(2):
                m0 = (2 * pair_index + i) * PIECE
                nc.sync.dma_start(out=pair[:, i, :, :], in_=traffic_rows[:, :, m0 : m0 + PIECE])
                ys.append(pair[:, i, :, :])

        def second_product(b, c):
            cols = slice(c * PIECE, (c + 1) * PIECE)
            for t in range(PACK):
                bank = banks[2 * c + t // 2]
                nc.tensor.matmul_mx(
                    out=bank[:, (t % 2) * PIECE : (t % 2 + 1) * PIECE],
                    lhsT=w4_w[:, b, 2 * P * t : 2 * P * (t + 1)].bitcast(FP4X4),
                    lhsT_scale=w4_s[:, b, P * t : P * (t + 1)],
                    rhs=x_w[b][:, cols].bitcast(FP8X4),
                    rhs_scale=x_s[b][:, cols],
                    start=(b == 0 and t % 2 == 0),
                    stop=(b == PASSES - 1 and t % 2 == 1),
                )

        for j in range(HALVES):
            cols = slice(j * BANK, (j + 1) * BANK)
            rounded = ring.tile([P, PACK * BANK], BF16, name="x_bf_wide", tag="wide", align_bytes=64)
            round_interleaved(nc.scalar.copy, rounded[:], x_first[:, :, cols])
            nc.vector.quantize_mx(out=x_w[0][:, cols].bitcast(FP8X4), scales=x_s[0][:, cols], in_=rounded[:])
        for c in range(PIECES):
            second_product(0, c)

        out_rows = out_0.rearrange("(p t) m -> p t m", t=PACK)
        out_words = out_1[0].rearrange("p m t -> p (m t)").bitcast(I32)

        def quantize_x(c):
            cols = slice(c * PIECE, (c + 1) * PIECE)
            rounded = ring.tile([P, PACK * PIECE], BF16, name="x_bf", tag="narrow", bufs=3, align_bytes=64)
            round_interleaved(nc.scalar.copy, rounded[:], x_piece[c % 2][:])
            nc.vector.quantize_mx(out=x_w[1][:, cols].bitcast(FP8X4), scales=x_s[1][:, cols], in_=rounded[:])
            second_product(1, c)

        def add_traffic(c):
            cols = slice(c * PIECE, (c + 1) * PIECE)
            for u in range(2):
                part = ys[c][:, 2 * u : 2 * u + 2, :].rearrange("p t m -> p (t m)")
                nc.vector.tensor_tensor(out=part, in0=banks[2 * c + u][:], in1=part, op=ADD)
            nc.sync.dma_start(out=out_rows[:, :, cols], in_=ys[c])

        def quantize_y(c):
            cols = slice(c * PIECE, (c + 1) * PIECE)
            rounded = ring.tile([P, PACK * PIECE], BF16, name="y_bf", tag="narrow", bufs=3, align_bytes=64)
            engine_copy = nc.vector.tensor_copy if c == PIECES - 1 else nc.scalar.copy
            round_interleaved(engine_copy, rounded[:], ys[c])
            nc.vector.quantize_mx(out=y_w[:, cols].bitcast(FP8X4), scales=y_s[:, cols], in_=rounded[:])
            nc.sync.dma_start(out=out_words[:, cols], in_=y_w[:, cols])

        fetch_x(0)
        for c in range(PIECES + 2):
            if c + 1 < PIECES:
                fetch_x(c + 1)
            if c < PIECES:
                quantize_x(c)
            if c >= 2:
                quantize_y(c - 2)
            if 1 <= c <= PIECES:
                add_traffic(c - 1)

        for q in range(QUADRANTS):
            queue = nc.scalar if q % 2 else nc.sync
            queue.dma_start(
                out=out_2[0, SCALE_ROWS * q : SCALE_ROWS * (q + 1), :].bitcast(I32),
                in_=y_s[QUADRANT * q : QUADRANT * q + SCALE_ROWS, :].bitcast(I32),
            )
